import numpy as np
import ml_dtypes


def mxq(x, axis, fmt="e4m3"):
    dtype, down = {"e4m3": (ml_dtypes.float8_e4m3fn, 7), "e5m2": (ml_dtypes.float8_e5m2, 14)}[fmt]
    v = np.moveaxis(np.asarray(x, np.float32).astype(ml_dtypes.bfloat16).astype(np.float64), axis, -1)
    blocks = v.reshape(v.shape[:-1] + (-1, 32))
    amax = np.abs(blocks).max(-1, keepdims=True)
    byte = np.maximum(np.where(amax > 0, np.frexp(amax)[1] - 1 + 127, 0) - down, 1)
    scale = np.exp2(byte - 127.0)
    codes = (blocks / scale).astype(np.float32).astype(dtype).astype(np.float64)
    return np.moveaxis((codes * scale).reshape(v.shape), -1, axis)


WIDE = False


def mx_kscale(k):
    if not WIDE:
        return np.ones(k)
    levels = np.array([10, -10, 5, -5, 0])
    if k % 512:
        return np.exp2(np.random.permutation(np.resize(levels, k // 32))).repeat(32)
    a = np.empty((k // 512, 16))
    for p in range(k // 512):
        a[p, :8] = np.random.permutation(np.resize(levels, 8))
        for g in range(8):
            far = levels[np.abs(levels - a[p, g]) >= 10]
            a[p, g + 8] = far[np.random.randint(len(far))]
    return np.exp2(a.ravel()).repeat(32)


def f64(x):
    return np.asarray(x).astype(np.float64)


def striped8(idx):
    return np.asarray(idx).reshape(8, -1, 16).transpose(0, 2, 1).reshape(128, -1).astype(np.uint16)


def unstriped8(offs):
    return offs.reshape(8, 16, -1).transpose(0, 2, 1).reshape(8, -1).astype(np.int64)


def pick8(x, idx, run):
    r = np.arange(len(x))
    return x[r[:, None], idx[r % (8 * run) // run]]


E2M1 = np.array([0.0, 0.5, 1.0, 1.5, 2.0, 3.0, 4.0, 6.0, -0.0, -0.5, -1.0, -1.5, -2.0, -3.0, -4.0, -6.0])


def pack_weight(w, fmt):
    k, n = w.shape
    w = f64(np.asarray(w, np.float32).astype(ml_dtypes.bfloat16)).reshape(k // 32, 32, n)
    amax = np.abs(w).max(1)
    if fmt == "e4m3":
        byte = np.frexp(amax)[1] - 1 + 127 - 7
    else:
        mant, ex = np.frexp(amax / 6.0)
        byte = np.where(mant > 0.5, ex, ex - 1) + 127
    byte = np.clip(np.where(amax > 0, byte, 1), 1, 254)
    scaled = (w * np.exp2(127.0 - byte)[:, None, :]).reshape(k, n).astype(np.float32)
    by_word = np.ascontiguousarray(scaled.reshape(k // 512, 128, 4, n).transpose(0, 1, 3, 2))
    if fmt == "e4m3":
        words = by_word.astype(ml_dtypes.float8_e4m3fn).view(np.uint8)
    else:
        c = by_word.astype(ml_dtypes.float4_e2m1fn).view(np.uint8) & 0xF
        words = (c[..., 0::2] | (c[..., 1::2] << 4)).reshape(k // 512, 128, 2 * n)
    return np.ascontiguousarray(words), np.ascontiguousarray(byte.astype(np.uint8).reshape(k // 512, 16, n))


def unpack_weight(words, scales, fmt):
    g, _, n = scales.shape
    words = np.ascontiguousarray(words).reshape(g, 128, n, -1)
    if fmt == "e4m3":
        vals = words.view(ml_dtypes.float8_e4m3fn).astype(np.float64)
    else:
        nib = np.empty((g, 128, n, 4), np.uint8)
        nib[..., 0::2] = words & 0xF
        nib[..., 1::2] = words >> 4
        vals = E2M1[nib]
    vals = vals * np.repeat(np.exp2(scales.astype(np.float64) - 127.0), 8, axis=1)[..., None]
    return vals.transpose(0, 1, 3, 2).reshape(g * 512, n)


D, K, T, I, Q = 512, 512, 1024, 512, 128


def setup_inputs():
    n = np.random.standard_normal
    idx = np.stack([np.random.permutation(T)[:I] for _ in range(8)])
    idx2 = np.stack([np.random.permutation(T)[:I] for _ in range(8)])
    idx3 = np.stack([np.random.permutation(T)[:I] for _ in range(8)])
    idx4 = np.stack([np.random.permutation(T)[:I] for _ in range(8)])
    idx5 = np.stack([np.random.permutation(T)[:I] for _ in range(8)])
    idx6 = np.stack([np.random.permutation(T)[:I] for _ in range(8)])
    fd = mx_kscale(D)
    fk = mx_kscale(K)
    wqp = pack_weight(n((D, K)) * 1.0 / np.sqrt(D) * fd[:, None] * fk, "e4m3")
    cachep = pack_weight(n((K, T)) * 1.0 / np.sqrt(K) / fk[:, None], "e2m1")
    tagsp = pack_weight(n((D, T)) * 0.5 / np.sqrt(D) * fd[:, None], "e4m3")
    return {
        "states": (n((D, Q)) * 0.95 / fd[:, None]).astype(np.float32),
        "wq_words": wqp[0],
        "wq_scales": wqp[1],
        "cache_words": cachep[0],
        "cache_scales": cachep[1],
        "tags_words": tagsp[0],
        "tags_scales": tagsp[1],
        "offs": striped8(idx),
        "offs2": striped8(idx2),
        "offs3": striped8(idx3),
        "offs4": striped8(idx4),
        "offs5": striped8(idx5),
        "offs6": striped8(idx6),
    }


def reference(states, wq_words, wq_scales, cache_words, cache_scales, tags_words, tags_scales, offs, offs2, offs3, offs4, offs5, offs6):
    idx = unstriped8(offs)
    idx2 = unstriped8(offs2)
    idx3 = unstriped8(offs3)
    idx4 = unstriped8(offs4)
    idx5 = unstriped8(offs5)
    idx6 = unstriped8(offs6)
    wqu = unpack_weight(wq_words, wq_scales, "e4m3")
    cacheu = unpack_weight(cache_words, cache_scales, "e2m1")
    tagsu = unpack_weight(tags_words, tags_scales, "e4m3")
    statesq = mxq(f64(states), 0, "e4m3")
    qv = wqu.T @ statesq
    qvq = mxq(qv, 0, "e4m3")
    a = qvq.T @ cacheu + statesq.T @ tagsu
    f1 = np.zeros((Q, T))
    f1[np.arange(Q)[:, None], idx2[np.arange(Q) % 128 // 16]] = pick8(a, idx, 16)
    f2 = np.zeros((Q, T))
    f2[np.arange(Q)[:, None], idx4[np.arange(Q) % 128 // 16]] = pick8(a, idx3, 16)
    f3 = np.zeros((Q, T))
    f3[np.arange(Q)[:, None], idx[np.arange(Q) % 128 // 16]] = pick8(a, idx5, 16)
    m1 = np.maximum(f1, f2)
    r = m1 - f3
    y = pick8(r, idx6, 16) + pick8(a, idx3, 16)
    return y

@@ -1,0 +1,191 @@
+from contextlib import ExitStack
+
+import concourse.mybir as mybir
+
+D, K, T, SLOTS, Q = 512, 512, 1024, 512, 128
+FLOPS = 2 * D * K * Q + 2 * K * Q * T + 2 * D * Q * T
+
+F32 = mybir.dt.float32
+BF16 = mybir.dt.bfloat16
+I32 = mybir.dt.int32
+U32 = mybir.dt.uint32
+U16 = mybir.dt.uint16
+U8 = mybir.dt.uint8
+FP8X4 = mybir.dt.float8_e4m3fn_x4
+FP4X4 = mybir.dt.float4_e2m1fn_x4
+COPY = mybir.ActivationFunctionType.Copy
+ALU = mybir.AluOpType
+
+P = 128
+PACK = 4
+QUADS = 4
+BANK_COLS = 256
+HALF = SLOTS // 2
+HALF_OFFS = HALF // 16
+
+
+def tile_attend_threewrites_parts_kernel(
+    tc, states, wq_words, wq_scales, cache_words, cache_scales, tags_words, tags_scales,
+    offs, offs2, offs3, offs4, offs5, offs6, out,
+):
+    nc = tc.nc
+    with ExitStack() as ctx:
+        sb = ctx.enter_context(tc.tile_pool(name="sb", bufs=1))
+        ps = ctx.enter_context(tc.psum_pool(name="ps", bufs=1))
+
+        def scale_tile(name, width):
+            t = sb.tile([P, QUADS * width], U8, name=name, align_bytes=64)
+            nc.vector.memset(t[:, 0:width].bitcast(I32), 0)
+            return t
+
+        def load_scales(t, rows, width):
+            nc.sync.dma_start(
+                t[0:4, :].bitcast(I32).rearrange("r (q n) -> r q n", q=QUADS),
+                rows[0].bitcast(I32).rearrange("(q r) n -> r q n", q=QUADS),
+            )
+
+        def spread_scales(t, width):
+            for q in range(1, QUADS):
+                nc.vector.tensor_copy(
+                    t[32 * q : 32 * q + 4, 0:width].bitcast(I32),
+                    t[0:4, q * width : (q + 1) * width].bitcast(I32),
+                )
+
+        wq_rows = scale_tile("wq_rows", K)
+        tags_plane = scale_tile("tags_plane", T)
+        cache_plane = scale_tile("cache_plane", T)
+
+        load_scales(wq_rows, wq_scales, K)
+        states_raw = sb.tile([P, PACK, Q], F32, name="states_raw")
+        nc.sync.dma_start(states_raw[:], states.rearrange("(p j) q -> p j q", j=PACK))
+        wq_raw = sb.tile([P, K], U32, name="wq_raw")
+        nc.sync.dma_start(wq_raw[:].bitcast(I32), wq_words[0].rearrange("p n t -> p (n t)").bitcast(I32))
+        load_scales(tags_plane, tags_scales, T)
+        load_scales(cache_plane, cache_scales, T)
+        tags_flat = tags_words[0].rearrange("p n t -> p (n t)").bitcast(I32)
+        tags_codes = []
+        for h in range(2):
+            t = sb.tile([P, T // 2], U32, name="tags_codes%d" % h, align_bytes=64)
+            nc.sync.dma_start(t[:].bitcast(I32), tags_flat[:, h * T // 2 : (h + 1) * T // 2])
+            tags_codes.append(t)
+        cache_codes = sb.tile([P, 2 * T], U8, name="cache_codes", align_bytes=64)
+        nc.sync.dma_start(cache_codes[:].bitcast(I32), cache_words[0].bitcast(I32))
+
+        lists = {}
+        for name, src in (("idx", offs), ("idx2", offs2), ("idx3", offs3), ("idx4", offs4), ("idx5", offs5), ("idx6", offs6)):
+            lists[name] = sb.tile([P, SLOTS // 16], U16, name=name)
+            nc.sync.dma_start(lists[name][:], src)
+
+        f1 = sb.tile([P, T], F32, name="f1")
+        f2 = sb.tile([P, T], F32, name="f2")
+        f3 = sb.tile([P, T], F32, name="f3")
+        for f in (f1, f2, f3):
+            nc.vector.memset(f[:], 0.0)
+
+        spread_scales(wq_rows, K)
+        wq_plane = sb.tile([P, K], U8, name="wq_plane", align_bytes=64)
+        nc.vector.tensor_copy(
+            wq_plane[:].rearrange("p (t m) -> p m t", t=PACK),
+            wq_rows[:, 0:K].rearrange("p (m t) -> p m t", t=PACK),
+        )
+
+        states_bf = sb.tile([P, Q * PACK], BF16, name="states_bf", align_bytes=64)
+        nc.scalar.activation(
+            states_bf[:].rearrange("p (c i j) -> p c j i", i=4, j=PACK),
+            states_raw[:].rearrange("p j (c i) -> p c j i", i=4),
+            COPY,
+        )
+        wq_by_t = wq_raw[:].rearrange("p (m t) -> p m t", t=PACK)
+        wq_lo = sb.tile([P, 2 * P], U32, name="wq_lo", align_bytes=64)
+        wq_hi = sb.tile([P, 2 * P], U32, name="wq_hi", align_bytes=64)
+        nc.vector.tensor_copy(wq_lo[:].rearrange("p (t m) -> p m t", t=2), wq_by_t[:, :, 0:2])
+        nc.scalar.copy(wq_hi[:].rearrange("p (t m) -> p m t", t=2), wq_by_t[:, :, 2:4])
+
+        states_codes = sb.tile([P, Q], U32, name="states_codes", align_bytes=64)
+        states_plane = sb.tile([P, Q], U8, name="states_plane", align_bytes=64)
+        nc.vector.quantize_mx(states_codes[:].bitcast(FP8X4), states_plane[:], states_bf[:])
+
+        qv_ps = ps.tile([P, PACK * Q], F32, name="qv_ps")
+        for t in range(PACK):
+            dealt = (wq_lo, wq_hi)[t // 2]
+            nc.tensor.matmul_mx(
+                qv_ps[:, t * Q : (t + 1) * Q],
+                lhsT=dealt[:, (t % 2) * P : (t % 2 + 1) * P].bitcast(FP8X4),
+                lhsT_scale=wq_plane[:, t * P : (t + 1) * P],
+                rhs=states_codes[:].bitcast(FP8X4),
+                rhs_scale=states_plane[:],
+                start=True,
+                stop=True,
+            )
+        qv_bf = sb.tile([P, Q * PACK], BF16, name="qv_bf", align_bytes=64)
+        nc.scalar.copy(
+            qv_bf[:].rearrange("p (q t) -> p q t", t=PACK),
+            qv_ps[:].rearrange("p (t q) -> p q t", t=PACK),
+        )
+
+        spread_scales(tags_plane, T)
+        spread_scales(cache_plane, T)
+
+        qv_codes = sb.tile([P, Q], U32, name="qv_codes", align_bytes=64)
+        qv_plane = sb.tile([P, Q], U8, name="qv_plane", align_bytes=64)
+        nc.vector.quantize_mx(qv_codes[:].bitcast(FP8X4), qv_plane[:], qv_bf[:])
+
+        n_banks = T // BANK_COLS
+        banks = [ps.tile([P, BANK_COLS], F32, name="score%d" % b) for b in range(n_banks)]
+        for b in range(n_banks):
+            c0 = b * BANK_COLS
+            within = c0 % (T // 2)
+            nc.tensor.matmul_mx(
+                banks[b][:],
+                lhsT=states_codes[:].bitcast(FP8X4),
+                lhsT_scale=states_plane[:],
+                rhs=tags_codes[c0 // (T // 2)][:, within : within + BANK_COLS].bitcast(FP8X4),
+                rhs_scale=tags_plane[:, c0 : c0 + BANK_COLS],
+                start=True,
+                stop=False,
+            )
+        a = sb.tile([P, T], F32, name="a")
+        for b in range(n_banks):
+            c0 = b * BANK_COLS
+            nc.tensor.matmul_mx(
+                banks[b][:],
+                lhsT=qv_codes[:].bitcast(FP8X4),
+                lhsT_scale=qv_plane[:],
+                rhs=cache_codes[:, 2 * c0 : 2 * (c0 + BANK_COLS)].bitcast(FP4X4),
+                rhs_scale=cache_plane[:, c0 : c0 + BANK_COLS],
+                start=False,
+                stop=True,
+            )
+            if b % 2 == 0:
+                nc.vector.tensor_copy(a[:, c0 : c0 + BANK_COLS], banks[b][:])
+            else:
+                nc.scalar.copy(a[:, c0 : c0 + BANK_COLS], banks[b][:])
+
+        def half_list(name, h):
+            return lists[name][:, h * HALF_OFFS : (h + 1) * HALF_OFFS]
+
+        g1 = [sb.tile([P, HALF], F32, name="g1_%d" % h) for h in range(2)]
+        g3 = sb.tile([P, SLOTS], F32, name="g3")
+        g5 = sb.tile([P, SLOTS], F32, name="g5")
+        nc.vector.tensor_copy(g1[0][:], a[:].indirect(half_list("idx", 0)))
+        nc.scalar.activation(f1[:].indirect(half_list("idx2", 0)), g1[0][:], COPY)
+        nc.vector.tensor_copy(g3[:], a[:].indirect(lists["idx3"][:]))
+        nc.scalar.activation(f2[:].indirect(lists["idx4"][:]), g3[:], COPY)
+        nc.vector.tensor_copy(g1[1][:], a[:].indirect(half_list("idx", 1)))
+        nc.scalar.activation(f1[:].indirect(half_list("idx2", 1)), g1[1][:], COPY)
+        nc.vector.tensor_copy(g5[:], a[:].indirect(lists["idx5"][:]))
+        nc.scalar.activation(f3[:].indirect(lists["idx"][:]), g5[:], COPY)
+
+        m1 = sb.tile([P, T], F32, name="m1")
+        nc.vector.tensor_tensor(m1[:], f1[:], f2[:], ALU.max)
+        r = sb.tile([P, T], F32, name="r")
+        nc.vector.tensor_tensor(r[:], m1[:], f3[:], ALU.subtract)
+
+        y0 = sb.tile([P, HALF], F32, name="y0")
+        y1 = sb.tile([P, HALF], F32, name="y1")
+        picked = sb.tile([P, HALF], F32, name="picked")
+        nc.scalar.activation(picked[:], r[:].indirect(half_list("idx6", 1)), COPY)
+        nc.vector.tensor_tensor(y0[:], r[:].indirect(half_list("idx6", 0)), g3[:, 0:HALF], ALU.add)
+        nc.sync.dma_start(out[:, 0:HALF], y0[:])
+        nc.vector.tensor_tensor(y1[:], picked[:], g3[:, HALF:SLOTS], ALU.add)
+        nc.sync.dma_start(out[:, HALF:SLOTS], y1[:])

@@ -19,7 +19,8 @@ ALU = mybir.AluOpType
 P = 128
 PACK = 4
 QUADS = 4
-BANK_COLS = 256
+BANK_COLS = (256, 256, 256, 128, 128)
+TAGS_ROW = 4
 HALF = SLOTS // 2
 HALF_OFFS = HALF // 16
 
@@ -33,35 +34,39 @@ def tile_attend_threewrites_parts_kernel(
         sb = ctx.enter_context(tc.tile_pool(name="sb", bufs=1))
         ps = ctx.enter_context(tc.psum_pool(name="ps", bufs=1))
 
-        def scale_tile(name, width):
-            t = sb.tile([P, QUADS * width], U8, name=name, align_bytes=64)
-            nc.vector.memset(t[:, 0:width].bitcast(I32), 0)
+        def scale_tile(name, width, engine):
+            t = sb.tile([64, 2 * width], U8, name=name)
+            engine.memset(t[:].bitcast(I32), 0)
             return t
 
-        def load_scales(t, rows, width):
-            nc.sync.dma_start(
-                t[0:4, :].bitcast(I32).rearrange("r (q n) -> r q n", q=QUADS),
-                rows[0].bitcast(I32).rearrange("(q r) n -> r q n", q=QUADS),
+        def load_scales(t, rows, first, odd):
+            by_quad = rows[0].bitcast(I32).rearrange("(h o r) n -> o r h n", h=2, o=2)
+            p0 = 32 * odd + first
+            nc.sync.dma_start(t[p0 : p0 + 4, :].bitcast(I32).rearrange("r (h n) -> r h n", h=2), by_quad[odd])
+
+        def spread_scales(plane, staged, width, half):
+            nc.vector.tensor_copy(
+                plane[64 * half : 64 * half + 64, 0:width].bitcast(I32),
+                staged[0:64, half * width : (half + 1) * width].bitcast(I32),
             )
 
-        def spread_scales(t, width):
-            for q in range(1, QUADS):
-                nc.vector.tensor_copy(
-                    t[32 * q : 32 * q + 4, 0:width].bitcast(I32),
-                    t[0:4, q * width : (q + 1) * width].bitcast(I32),
-                )
+        tags_rows = scale_tile("tags_rows", T, nc.vector)
+        cache_rows = scale_tile("cache_rows", T, nc.gpsimd)
+        wq_spread = sb.tile([P, K], U8, name="wq_spread")
+        nc.vector.memset(wq_spread[:].bitcast(I32), 0)
 
-        wq_rows = scale_tile("wq_rows", K)
-        tags_plane = scale_tile("tags_plane", T)
-        cache_plane = scale_tile("cache_plane", T)
-
-        load_scales(wq_rows, wq_scales, K)
+        wq_rows = sb.tile([4, QUADS * K], U8, name="wq_rows")
+        nc.sync.dma_start(
+            wq_rows[:].bitcast(I32).rearrange("r (q n) -> r q n", q=QUADS),
+            wq_scales[0].bitcast(I32).rearrange("(q r) n -> r q n", q=QUADS),
+        )
         states_raw = sb.tile([P, PACK, Q], F32, name="states_raw")
         nc.sync.dma_start(states_raw[:], states.rearrange("(p j) q -> p j q", j=PACK))
-        wq_raw = sb.tile([P, K], U32, name="wq_raw")
+        wq_raw = sb.tile([P, K], U32, name="wq_raw", tag="wq_then_planes", align_bytes=64)
         nc.sync.dma_start(wq_raw[:].bitcast(I32), wq_words[0].rearrange("p n t -> p (n t)").bitcast(I32))
-        load_scales(tags_plane, tags_scales, T)
-        load_scales(cache_plane, cache_scales, T)
+        for odd in range(2):
+            load_scales(tags_rows, tags_scales, TAGS_ROW, odd)
+            load_scales(cache_rows, cache_scales, 0, odd)
         tags_flat = tags_words[0].rearrange("p n t -> p (n t)").bitcast(I32)
         tags_codes = []
         for h in range(2):
@@ -78,15 +83,18 @@ def tile_attend_threewrites_parts_kernel(
 
         f1 = sb.tile([P, T], F32, name="f1")
         f2 = sb.tile([P, T], F32, name="f2")
-        f3 = sb.tile([P, T], F32, name="f3")
-        for f in (f1, f2, f3):
+        for f in (f1, f2):
             nc.vector.memset(f[:], 0.0)
 
-        spread_scales(wq_rows, K)
+        for q in range(QUADS):
+            nc.vector.tensor_copy(
+                wq_spread[32 * q : 32 * q + 4, :].bitcast(I32),
+                wq_rows[:, q * K : (q + 1) * K].bitcast(I32),
+            )
         wq_plane = sb.tile([P, K], U8, name="wq_plane", align_bytes=64)
         nc.vector.tensor_copy(
             wq_plane[:].rearrange("p (t m) -> p m t", t=PACK),
-            wq_rows[:, 0:K].rearrange("p (m t) -> p m t", t=PACK),
+            wq_spread[:].rearrange("p (m t) -> p m t", t=PACK),
         )
 
         states_bf = sb.tile([P, Q * PACK], BF16, name="states_bf", align_bytes=64)
@@ -98,7 +106,7 @@ def tile_attend_threewrites_parts_kernel(
         wq_by_t = wq_raw[:].rearrange("p (m t) -> p m t", t=PACK)
         wq_lo = sb.tile([P, 2 * P], U32, name="wq_lo", align_bytes=64)
         wq_hi = sb.tile([P, 2 * P], U32, name="wq_hi", align_bytes=64)
-        nc.vector.tensor_copy(wq_lo[:].rearrange("p (t m) -> p m t", t=2), wq_by_t[:, :, 0:2])
+        nc.scalar.copy(wq_lo[:].rearrange("p (t m) -> p m t", t=2), wq_by_t[:, :, 0:2])
         nc.scalar.copy(wq_hi[:].rearrange("p (t m) -> p m t", t=2), wq_by_t[:, :, 2:4])
 
         states_codes = sb.tile([P, Q], U32, name="states_codes", align_bytes=64)
@@ -123,48 +131,51 @@ def tile_attend_threewrites_parts_kernel(
             qv_ps[:].rearrange("p (t q) -> p q t", t=PACK),
         )
 
-        spread_scales(tags_plane, T)
-        spread_scales(cache_plane, T)
+        key_planes = sb.tile([P, 2 * T], U8, name="key_planes", tag="wq_then_planes", align_bytes=64)
+        tags_plane = key_planes[:, 0:T]
+        cache_plane = key_planes[:, T : 2 * T]
+        for half in (0, 1):
+            spread_scales(tags_plane, tags_rows, T, half)
+        for half in (1, 0):
+            spread_scales(cache_plane, cache_rows, T, half)
 
         qv_codes = sb.tile([P, Q], U32, name="qv_codes", align_bytes=64)
         qv_plane = sb.tile([P, Q], U8, name="qv_plane", align_bytes=64)
         nc.vector.quantize_mx(qv_codes[:].bitcast(FP8X4), qv_plane[:], qv_bf[:])
 
-        n_banks = T // BANK_COLS
-        banks = [ps.tile([P, BANK_COLS], F32, name="score%d" % b) for b in range(n_banks)]
-        for b in range(n_banks):
-            c0 = b * BANK_COLS
+        starts = [sum(BANK_COLS[:b]) for b in range(len(BANK_COLS))]
+        banks = [ps.tile([P, n], F32, name="score%d" % b) for b, n in enumerate(BANK_COLS)]
+        for bank, c0, n in zip(banks, starts, BANK_COLS):
             within = c0 % (T // 2)
             nc.tensor.matmul_mx(
-                banks[b][:],
+                bank[:],
                 lhsT=states_codes[:].bitcast(FP8X4),
                 lhsT_scale=states_plane[:],
-                rhs=tags_codes[c0 // (T // 2)][:, within : within + BANK_COLS].bitcast(FP8X4),
-                rhs_scale=tags_plane[:, c0 : c0 + BANK_COLS],
+                rhs=tags_codes[c0 // (T // 2)][:, within : within + n].bitcast(FP8X4),
+                rhs_scale=tags_plane[TAGS_ROW:P, c0 : c0 + n],
                 start=True,
                 stop=False,
             )
         a = sb.tile([P, T], F32, name="a")
-        for b in range(n_banks):
-            c0 = b * BANK_COLS
+        for b, (bank, c0, n) in enumerate(zip(banks, starts, BANK_COLS)):
             nc.tensor.matmul_mx(
-                banks[b][:],
+                bank[:],
                 lhsT=qv_codes[:].bitcast(FP8X4),
                 lhsT_scale=qv_plane[:],
-                rhs=cache_codes[:, 2 * c0 : 2 * (c0 + BANK_COLS)].bitcast(FP4X4),
-                rhs_scale=cache_plane[:, c0 : c0 + BANK_COLS],
+                rhs=cache_codes[:, 2 * c0 : 2 * (c0 + n)].bitcast(FP4X4),
+                rhs_scale=cache_plane[:, c0 : c0 + n],
                 start=False,
                 stop=True,
             )
-            if b % 2 == 0:
-                nc.vector.tensor_copy(a[:, c0 : c0 + BANK_COLS], banks[b][:])
+            if b in (0, 2):
+                nc.vector.tensor_copy(a[:, c0 : c0 + n], bank[:])
             else:
-                nc.scalar.copy(a[:, c0 : c0 + BANK_COLS], banks[b][:])
+                nc.scalar.copy(a[:, c0 : c0 + n], bank[:])
 
         def half_list(name, h):
             return lists[name][:, h * HALF_OFFS : (h + 1) * HALF_OFFS]
 
-        g1 = [sb.tile([P, HALF], F32, name="g1_%d" % h) for h in range(2)]
+        g1 = [sb.tile([P, HALF], F32, name="g1_0", tag="g1_then_f3"), sb.tile([P, HALF], F32, name="g1_1")]
         g3 = sb.tile([P, SLOTS], F32, name="g3")
         g5 = sb.tile([P, SLOTS], F32, name="g5")
         nc.vector.tensor_copy(g1[0][:], a[:].indirect(half_list("idx", 0)))
@@ -174,6 +185,8 @@ def tile_attend_threewrites_parts_kernel(
         nc.vector.tensor_copy(g1[1][:], a[:].indirect(half_list("idx", 1)))
         nc.scalar.activation(f1[:].indirect(half_list("idx2", 1)), g1[1][:], COPY)
         nc.vector.tensor_copy(g5[:], a[:].indirect(lists["idx5"][:]))
+        f3 = sb.tile([P, T], F32, name="f3", tag="g1_then_f3")
+        nc.vector.memset(f3[:], 0.0)
         nc.scalar.activation(f3[:].indirect(lists["idx"][:]), g5[:], COPY)
 
         m1 = sb.tile([P, T], F32, name="m1")

@@ -82,9 +82,7 @@ def tile_attend_threewrites_parts_kernel(
             nc.sync.dma_start(lists[name][:], src)
 
         f1 = sb.tile([P, T], F32, name="f1")
-        f2 = sb.tile([P, T], F32, name="f2")
-        for f in (f1, f2):
-            nc.vector.memset(f[:], 0.0)
+        nc.vector.memset(f1[:], 0.0)
 
         for q in range(QUADS):
             nc.vector.tensor_copy(
@@ -97,7 +95,7 @@ def tile_attend_threewrites_parts_kernel(
             wq_spread[:].rearrange("p (m t) -> p m t", t=PACK),
         )
 
-        states_bf = sb.tile([P, Q * PACK], BF16, name="states_bf", align_bytes=64)
+        states_bf = sb.tile([P, Q * PACK], BF16, name="states_bf", tag="states_then_plane", align_bytes=64)
         nc.scalar.activation(
             states_bf[:].rearrange("p (c i j) -> p c j i", i=4, j=PACK),
             states_raw[:].rearrange("p j (c i) -> p c j i", i=4),
@@ -125,15 +123,14 @@ def tile_attend_threewrites_parts_kernel(
                 start=True,
                 stop=True,
             )
-        qv_bf = sb.tile([P, Q * PACK], BF16, name="qv_bf", align_bytes=64)
+        qv_bf = sb.tile([P, Q * PACK], BF16, name="qv_bf", tag="qv_then_f2", align_bytes=64)
         nc.scalar.copy(
             qv_bf[:].rearrange("p (q t) -> p q t", t=PACK),
             qv_ps[:].rearrange("p (t q) -> p q t", t=PACK),
         )
 
-        key_planes = sb.tile([P, 2 * T], U8, name="key_planes", tag="wq_then_planes", align_bytes=64)
-        tags_plane = key_planes[:, 0:T]
-        cache_plane = key_planes[:, T : 2 * T]
+        tags_plane = sb.tile([P, T], U8, name="tags_plane", tag="states_then_plane", align_bytes=64)
+        cache_plane = sb.tile([P, T], U8, name="cache_plane", tag="wq_then_planes", align_bytes=64)
         for half in (0, 1):
             spread_scales(tags_plane, tags_rows, T, half)
         for half in (1, 0):
@@ -142,6 +139,9 @@ def tile_attend_threewrites_parts_kernel(
         qv_codes = sb.tile([P, Q], U32, name="qv_codes", align_bytes=64)
         qv_plane = sb.tile([P, Q], U8, name="qv_plane", align_bytes=64)
         nc.vector.quantize_mx(qv_codes[:].bitcast(FP8X4), qv_plane[:], qv_bf[:])
+
+        f2 = sb.tile([P, T], F32, name="f2", tag="qv_then_f2", align_bytes=64)
+        nc.vector.memset(f2[:], 0.0)
 
         starts = [sum(BANK_COLS[:b]) for b in range(len(BANK_COLS))]
         banks = [ps.tile([P, n], F32, name="score%d" % b) for b, n in enumerate(BANK_COLS)]
@@ -167,7 +167,7 @@ def tile_attend_threewrites_parts_kernel(
                 start=False,
                 stop=True,
             )
-            if b in (0, 2):
+            if b % 2 == 1:
                 nc.vector.tensor_copy(a[:, c0 : c0 + n], bank[:])
             else:
                 nc.scalar.copy(a[:, c0 : c0 + n], bank[:])

@@ -34,11 +34,6 @@ def tile_attend_threewrites_parts_kernel(
         sb = ctx.enter_context(tc.tile_pool(name="sb", bufs=1))
         ps = ctx.enter_context(tc.psum_pool(name="ps", bufs=1))
 
-        def scale_tile(name, width, engine):
-            t = sb.tile([64, 2 * width], U8, name=name)
-            engine.memset(t[:].bitcast(I32), 0)
-            return t
-
         def load_scales(t, rows, first, odd):
             by_quad = rows[0].bitcast(I32).rearrange("(h o r) n -> o r h n", h=2, o=2)
             p0 = 32 * odd + first
@@ -50,8 +45,8 @@ def tile_attend_threewrites_parts_kernel(
                 staged[0:64, half * width : (half + 1) * width].bitcast(I32),
             )
 
-        tags_rows = scale_tile("tags_rows", T, nc.vector)
-        cache_rows = scale_tile("cache_rows", T, nc.gpsimd)
+        key_rows = sb.tile([64, 2 * T], U8, name="key_rows", tag="rows_then_f2")
+        nc.vector.memset(key_rows[:].bitcast(I32), 0)
         wq_spread = sb.tile([P, K], U8, name="wq_spread")
         nc.vector.memset(wq_spread[:].bitcast(I32), 0)
 
@@ -62,11 +57,11 @@ def tile_attend_threewrites_parts_kernel(
         )
         states_raw = sb.tile([P, PACK, Q], F32, name="states_raw")
         nc.sync.dma_start(states_raw[:], states.rearrange("(p j) q -> p j q", j=PACK))
-        wq_raw = sb.tile([P, K], U32, name="wq_raw", tag="wq_then_planes", align_bytes=64)
+        wq_raw = sb.tile([P, K], U32, name="wq_raw")
         nc.sync.dma_start(wq_raw[:].bitcast(I32), wq_words[0].rearrange("p n t -> p (n t)").bitcast(I32))
         for odd in range(2):
-            load_scales(tags_rows, tags_scales, TAGS_ROW, odd)
-            load_scales(cache_rows, cache_scales, 0, odd)
+            load_scales(key_rows, tags_scales, TAGS_ROW, odd)
+            load_scales(key_rows, cache_scales, 0, odd)
         tags_flat = tags_words[0].rearrange("p n t -> p (n t)").bitcast(I32)
         tags_codes = []
         for h in range(2):
@@ -123,25 +118,21 @@ def tile_attend_threewrites_parts_kernel(
                 start=True,
                 stop=True,
             )
-        qv_bf = sb.tile([P, Q * PACK], BF16, name="qv_bf", tag="qv_then_f2", align_bytes=64)
+        qv_bf = sb.tile([P, Q * PACK], BF16, name="qv_bf", align_bytes=64)
         nc.scalar.copy(
             qv_bf[:].rearrange("p (q t) -> p q t", t=PACK),
             qv_ps[:].rearrange("p (t q) -> p q t", t=PACK),
         )
 
-        tags_plane = sb.tile([P, T], U8, name="tags_plane", tag="states_then_plane", align_bytes=64)
-        cache_plane = sb.tile([P, T], U8, name="cache_plane", tag="wq_then_planes", align_bytes=64)
-        for half in (0, 1):
-            spread_scales(tags_plane, tags_rows, T, half)
-        for half in (1, 0):
-            spread_scales(cache_plane, cache_rows, T, half)
+        key_planes = sb.tile([P, T], U8, name="key_planes", tag="states_then_plane", align_bytes=64)
+        for half in range(2):
+            spread_scales(key_planes, key_rows, T, half)
+        f2 = sb.tile([P, T], F32, name="f2", tag="rows_then_f2")
+        nc.vector.memset(f2[:], 0.0)
 
         qv_codes = sb.tile([P, Q], U32, name="qv_codes", align_bytes=64)
         qv_plane = sb.tile([P, Q], U8, name="qv_plane", align_bytes=64)
         nc.vector.quantize_mx(qv_codes[:].bitcast(FP8X4), qv_plane[:], qv_bf[:])
-
-        f2 = sb.tile([P, T], F32, name="f2", tag="qv_then_f2", align_bytes=64)
-        nc.vector.memset(f2[:], 0.0)
 
         starts = [sum(BANK_COLS[:b]) for b in range(len(BANK_COLS))]
         banks = [ps.tile([P, n], F32, name="score%d" % b) for b, n in enumerate(BANK_COLS)]
@@ -152,7 +143,7 @@ def tile_attend_threewrites_parts_kernel(
                 lhsT=states_codes[:].bitcast(FP8X4),
                 lhsT_scale=states_plane[:],
                 rhs=tags_codes[c0 // (T // 2)][:, within : within + n].bitcast(FP8X4),
-                rhs_scale=tags_plane[TAGS_ROW:P, c0 : c0 + n],
+                rhs_scale=key_planes[TAGS_ROW:P, c0 : c0 + n],
                 start=True,
                 stop=False,
             )
@@ -163,11 +154,11 @@ def tile_attend_threewrites_parts_kernel(
                 lhsT=qv_codes[:].bitcast(FP8X4),
                 lhsT_scale=qv_plane[:],
                 rhs=cache_codes[:, 2 * c0 : 2 * (c0 + n)].bitcast(FP4X4),
-                rhs_scale=cache_plane[:, c0 : c0 + n],
+                rhs_scale=key_planes[:, c0 : c0 + n],
                 start=False,
                 stop=True,
             )
-            if b % 2 == 1:
+            if b in (0, 2):
                 nc.vector.tensor_copy(a[:, c0 : c0 + n], bank[:])
             else:
                 nc.scalar.copy(a[:, c0 : c0 + n], bank[:])

@@ -1,6 +1,7 @@
 from contextlib import ExitStack
 
 import concourse.mybir as mybir
+from concourse.masks import make_identity
 
 D, K, T, SLOTS, Q = 512, 512, 1024, 512, 128
 FLOPS = 2 * D * K * Q + 2 * K * Q * T + 2 * D * Q * T
@@ -19,10 +20,16 @@ ALU = mybir.AluOpType
 P = 128
 PACK = 4
 QUADS = 4
+QUAD = P // QUADS
+LIVE = 4
+TAGS_FIRST = 4
+T_HALF = T // 2
 BANK_COLS = (256, 256, 256, 128, 128)
-TAGS_ROW = 4
 HALF = SLOTS // 2
-HALF_OFFS = HALF // 16
+LIST_COLS = SLOTS // 16
+PAIR = 2 * P
+VECTOR_PAIRS = 3
+VECTOR_COLS = VECTOR_PAIRS * PAIR
 
 
 def tile_attend_threewrites_parts_kernel(
@@ -34,99 +41,101 @@ def tile_attend_threewrites_parts_kernel(
         sb = ctx.enter_context(tc.tile_pool(name="sb", bufs=1))
         ps = ctx.enter_context(tc.psum_pool(name="ps", bufs=1))
 
-        def load_scales(t, rows, first, odd):
-            by_quad = rows[0].bitcast(I32).rearrange("(h o r) n -> o r h n", h=2, o=2)
-            p0 = 32 * odd + first
-            nc.sync.dma_start(t[p0 : p0 + 4, :].bitcast(I32).rearrange("r (h n) -> r h n", h=2), by_quad[odd])
-
-        def spread_scales(plane, staged, width, half):
-            nc.vector.tensor_copy(
-                plane[64 * half : 64 * half + 64, 0:width].bitcast(I32),
-                staged[0:64, half * width : (half + 1) * width].bitcast(I32),
-            )
-
-        key_rows = sb.tile([64, 2 * T], U8, name="key_rows", tag="rows_then_f2")
+        key_rows = sb.tile([P // 2, 2 * T], U8, name="key_rows", tag="rows_then_f2")
         nc.vector.memset(key_rows[:].bitcast(I32), 0)
         wq_spread = sb.tile([P, K], U8, name="wq_spread")
         nc.vector.memset(wq_spread[:].bitcast(I32), 0)
 
-        wq_rows = sb.tile([4, QUADS * K], U8, name="wq_rows")
+        wq_rows = sb.tile([LIVE, QUADS * K], U8, name="wq_rows")
         nc.sync.dma_start(
-            wq_rows[:].bitcast(I32).rearrange("r (q n) -> r q n", q=QUADS),
-            wq_scales[0].bitcast(I32).rearrange("(q r) n -> r q n", q=QUADS),
+            wq_rows[:].bitcast(I32).rearrange("s (u n) -> s u n", u=QUADS),
+            wq_scales[0].bitcast(I32).rearrange("(u s) n -> s u n", u=QUADS),
         )
         states_raw = sb.tile([P, PACK, Q], F32, name="states_raw")
         nc.sync.dma_start(states_raw[:], states.rearrange("(p j) q -> p j q", j=PACK))
         wq_raw = sb.tile([P, K], U32, name="wq_raw")
-        nc.sync.dma_start(wq_raw[:].bitcast(I32), wq_words[0].rearrange("p n t -> p (n t)").bitcast(I32))
+        nc.sync.dma_start(wq_raw[:].bitcast(I32), wq_words[0].rearrange("p n j -> p (n j)").bitcast(I32))
         for odd in range(2):
-            load_scales(key_rows, tags_scales, TAGS_ROW, odd)
-            load_scales(key_rows, cache_scales, 0, odd)
-        tags_flat = tags_words[0].rearrange("p n t -> p (n t)").bitcast(I32)
+            for scales, first in ((tags_scales, TAGS_FIRST), (cache_scales, 0)):
+                by_quad = scales[0].bitcast(I32).rearrange("(h o s) n -> o s h n", h=2, o=2)
+                p0 = QUAD * odd + first
+                nc.sync.dma_start(
+                    key_rows[p0 : p0 + LIVE, :].bitcast(I32).rearrange("s (h n) -> s h n", h=2), by_quad[odd]
+                )
+        tags_flat = tags_words[0].rearrange("p n j -> p (n j)").bitcast(I32)
         tags_codes = []
         for h in range(2):
-            t = sb.tile([P, T // 2], U32, name="tags_codes%d" % h, align_bytes=64)
-            nc.sync.dma_start(t[:].bitcast(I32), tags_flat[:, h * T // 2 : (h + 1) * T // 2])
-            tags_codes.append(t)
-        cache_codes = sb.tile([P, 2 * T], U8, name="cache_codes", align_bytes=64)
-        nc.sync.dma_start(cache_codes[:].bitcast(I32), cache_words[0].bitcast(I32))
-
+            codes = sb.tile([P, T_HALF], U32, name="tags_codes%d" % h, align_bytes=64)
+            nc.sync.dma_start(codes[:].bitcast(I32), tags_flat[:, h * T_HALF : (h + 1) * T_HALF])
+            tags_codes.append(codes)
+        cache_codes = []
+        for h in range(2):
+            codes = sb.tile([P, 2 * T_HALF], U8, name="cache_codes%d" % h, align_bytes=64)
+            nc.sync.dma_start(
+                codes[:].bitcast(I32), cache_words[0][:, 2 * h * T_HALF : 2 * (h + 1) * T_HALF].bitcast(I32)
+            )
+            cache_codes.append(codes)
         lists = {}
-        for name, src in (("idx", offs), ("idx2", offs2), ("idx3", offs3), ("idx4", offs4), ("idx5", offs5), ("idx6", offs6)):
-            lists[name] = sb.tile([P, SLOTS // 16], U16, name=name)
+        for name, src in (
+            ("idx", offs), ("idx3", offs3), ("idx2", offs2), ("idx4", offs4), ("idx5", offs5), ("idx6", offs6),
+        ):
+            lists[name] = sb.tile([P, LIST_COLS], U16, name=name)
             nc.sync.dma_start(lists[name][:], src)
 
         f1 = sb.tile([P, T], F32, name="f1")
         nc.vector.memset(f1[:], 0.0)
+        ident = sb.tile([P, P], F32, name="ident")
+        make_identity(nc, ident[:])
 
-        for q in range(QUADS):
+        for u in range(QUADS):
             nc.vector.tensor_copy(
-                wq_spread[32 * q : 32 * q + 4, :].bitcast(I32),
-                wq_rows[:, q * K : (q + 1) * K].bitcast(I32),
+                wq_spread[QUAD * u : QUAD * u + LIVE, :].bitcast(I32),
+                wq_rows[:, u * K : (u + 1) * K].bitcast(I32),
             )
         wq_plane = sb.tile([P, K], U8, name="wq_plane", align_bytes=64)
         nc.vector.tensor_copy(
-            wq_plane[:].rearrange("p (t m) -> p m t", t=PACK),
-            wq_spread[:].rearrange("p (m t) -> p m t", t=PACK),
+            wq_plane[:].rearrange("p (j m) -> p m j", j=PACK),
+            wq_spread[:].rearrange("p (m j) -> p m j", j=PACK),
         )
 
-        states_bf = sb.tile([P, Q * PACK], BF16, name="states_bf", tag="states_then_plane", align_bytes=64)
+        states_bf = sb.tile([P, Q * PACK], BF16, name="states_bf", tag="states_then_planes", align_bytes=64)
         nc.scalar.activation(
             states_bf[:].rearrange("p (c i j) -> p c j i", i=4, j=PACK),
             states_raw[:].rearrange("p j (c i) -> p c j i", i=4),
             COPY,
         )
-        wq_by_t = wq_raw[:].rearrange("p (m t) -> p m t", t=PACK)
-        wq_lo = sb.tile([P, 2 * P], U32, name="wq_lo", align_bytes=64)
-        wq_hi = sb.tile([P, 2 * P], U32, name="wq_hi", align_bytes=64)
-        nc.scalar.copy(wq_lo[:].rearrange("p (t m) -> p m t", t=2), wq_by_t[:, :, 0:2])
-        nc.scalar.copy(wq_hi[:].rearrange("p (t m) -> p m t", t=2), wq_by_t[:, :, 2:4])
+        wq_by_place = wq_raw[:].rearrange("p (m j) -> p m j", j=PACK)
+        wq_dealt = [sb.tile([P, 2 * P], U32, name="wq_dealt%d" % h, align_bytes=64) for h in range(2)]
+        for h in range(2):
+            nc.scalar.copy(wq_dealt[h][:].rearrange("p (j m) -> p m j", j=2), wq_by_place[:, :, 2 * h : 2 * h + 2])
 
         states_codes = sb.tile([P, Q], U32, name="states_codes", align_bytes=64)
         states_plane = sb.tile([P, Q], U8, name="states_plane", align_bytes=64)
         nc.vector.quantize_mx(states_codes[:].bitcast(FP8X4), states_plane[:], states_bf[:])
 
         qv_ps = ps.tile([P, PACK * Q], F32, name="qv_ps")
-        for t in range(PACK):
-            dealt = (wq_lo, wq_hi)[t // 2]
+        for j in range(PACK):
             nc.tensor.matmul_mx(
-                qv_ps[:, t * Q : (t + 1) * Q],
-                lhsT=dealt[:, (t % 2) * P : (t % 2 + 1) * P].bitcast(FP8X4),
-                lhsT_scale=wq_plane[:, t * P : (t + 1) * P],
+                qv_ps[:, j * Q : (j + 1) * Q],
+                lhsT=wq_dealt[j // 2][:, (j % 2) * P : (j % 2 + 1) * P].bitcast(FP8X4),
+                lhsT_scale=wq_plane[:, j * P : (j + 1) * P],
                 rhs=states_codes[:].bitcast(FP8X4),
                 rhs_scale=states_plane[:],
                 start=True,
                 stop=True,
             )
-        qv_bf = sb.tile([P, Q * PACK], BF16, name="qv_bf", align_bytes=64)
+        qv_bf = sb.tile([P, Q * PACK], BF16, name="qv_bf", tag="qv_then_f3", align_bytes=64)
         nc.scalar.copy(
-            qv_bf[:].rearrange("p (q t) -> p q t", t=PACK),
-            qv_ps[:].rearrange("p (t q) -> p q t", t=PACK),
+            qv_bf[:].rearrange("p (q j) -> p q j", j=PACK),
+            qv_ps[:].rearrange("p (j q) -> p q j", j=PACK),
         )
 
-        key_planes = sb.tile([P, T], U8, name="key_planes", tag="states_then_plane", align_bytes=64)
-        for half in range(2):
-            spread_scales(key_planes, key_rows, T, half)
+        key_planes = sb.tile([P, T], U8, name="key_planes", tag="states_then_planes", align_bytes=64)
+        for h in range(2):
+            nc.vector.tensor_copy(
+                key_planes[h * P // 2 : (h + 1) * P // 2, :].bitcast(I32),
+                key_rows[:, h * T : (h + 1) * T].bitcast(I32),
+            )
         f2 = sb.tile([P, T], F32, name="f2", tag="rows_then_f2")
         nc.vector.memset(f2[:], 0.0)
 
@@ -134,62 +143,90 @@ def tile_attend_threewrites_parts_kernel(
         qv_plane = sb.tile([P, Q], U8, name="qv_plane", align_bytes=64)
         nc.vector.quantize_mx(qv_codes[:].bitcast(FP8X4), qv_plane[:], qv_bf[:])
 
+        f3 = sb.tile([P, T], F32, name="f3", tag="qv_then_f3", align_bytes=64)
+        nc.vector.memset(f3[:], 0.0)
+
         starts = [sum(BANK_COLS[:b]) for b in range(len(BANK_COLS))]
-        banks = [ps.tile([P, n], F32, name="score%d" % b) for b, n in enumerate(BANK_COLS)]
+        banks = [ps.tile([P, n], F32, name="score%d" % b, tag="bank%d" % b) for b, n in enumerate(BANK_COLS)]
         for bank, c0, n in zip(banks, starts, BANK_COLS):
-            within = c0 % (T // 2)
+            h, within = divmod(c0, T_HALF)
             nc.tensor.matmul_mx(
                 bank[:],
                 lhsT=states_codes[:].bitcast(FP8X4),
                 lhsT_scale=states_plane[:],
-                rhs=tags_codes[c0 // (T // 2)][:, within : within + n].bitcast(FP8X4),
-                rhs_scale=key_planes[TAGS_ROW:P, c0 : c0 + n],
+                rhs=tags_codes[h][:, within : within + n].bitcast(FP8X4),
+                rhs_scale=key_planes[TAGS_FIRST:P, c0 : c0 + n],
                 start=True,
                 stop=False,
             )
         a = sb.tile([P, T], F32, name="a")
         for b, (bank, c0, n) in enumerate(zip(banks, starts, BANK_COLS)):
+            h, within = divmod(c0, T_HALF)
             nc.tensor.matmul_mx(
                 bank[:],
                 lhsT=qv_codes[:].bitcast(FP8X4),
                 lhsT_scale=qv_plane[:],
-                rhs=cache_codes[:, 2 * c0 : 2 * (c0 + n)].bitcast(FP4X4),
+                rhs=cache_codes[h][:, 2 * within : 2 * (within + n)].bitcast(FP4X4),
                 rhs_scale=key_planes[:, c0 : c0 + n],
                 start=False,
                 stop=True,
             )
-            if b in (0, 2):
+            if b % 2 == 1:
                 nc.vector.tensor_copy(a[:, c0 : c0 + n], bank[:])
             else:
                 nc.scalar.copy(a[:, c0 : c0 + n], bank[:])
 
         def half_list(name, h):
-            return lists[name][:, h * HALF_OFFS : (h + 1) * HALF_OFFS]
+            return lists[name][:, h * LIST_COLS // 2 : (h + 1) * LIST_COLS // 2]
 
-        g1 = [sb.tile([P, HALF], F32, name="g1_0", tag="g1_then_f3"), sb.tile([P, HALF], F32, name="g1_1")]
-        g3 = sb.tile([P, SLOTS], F32, name="g3")
-        g5 = sb.tile([P, SLOTS], F32, name="g5")
-        nc.vector.tensor_copy(g1[0][:], a[:].indirect(half_list("idx", 0)))
-        nc.scalar.activation(f1[:].indirect(half_list("idx2", 0)), g1[0][:], COPY)
-        nc.vector.tensor_copy(g3[:], a[:].indirect(lists["idx3"][:]))
-        nc.scalar.activation(f2[:].indirect(lists["idx4"][:]), g3[:], COPY)
-        nc.vector.tensor_copy(g1[1][:], a[:].indirect(half_list("idx", 1)))
-        nc.scalar.activation(f1[:].indirect(half_list("idx2", 1)), g1[1][:], COPY)
-        nc.vector.tensor_copy(g5[:], a[:].indirect(lists["idx5"][:]))
-        f3 = sb.tile([P, T], F32, name="f3", tag="g1_then_f3")
-        nc.vector.memset(f3[:], 0.0)
-        nc.scalar.activation(f3[:].indirect(lists["idx"][:]), g5[:], COPY)
+        by_idx3 = sb.tile([P, SLOTS], F32, name="by_idx3")
+        by_idx5 = sb.tile([P, SLOTS], F32, name="by_idx5")
+        by_idx_first = sb.tile([P, HALF], F32, name="by_idx_first", tag="by_idx")
+        nc.vector.tensor_copy(by_idx_first[:], a[:].indirect(half_list("idx", 0)))
+        nc.scalar.activation(f1[:].indirect(half_list("idx2", 0)), by_idx_first[:], COPY)
+        nc.vector.tensor_copy(by_idx3[:], a[:].indirect(lists["idx3"][:]))
+        nc.scalar.activation(f2[:].indirect(lists["idx4"][:]), by_idx3[:], COPY)
+        by_idx_second = sb.tile([P, HALF], F32, name="by_idx_second", tag="by_idx")
+        nc.vector.tensor_copy(by_idx_second[:], a[:].indirect(half_list("idx", 1)))
+        nc.scalar.activation(f1[:].indirect(half_list("idx2", 1)), by_idx_second[:], COPY)
+        nc.vector.tensor_copy(by_idx5[:], a[:].indirect(lists["idx5"][:]))
+        nc.scalar.activation(f3[:].indirect(lists["idx"][:]), by_idx5[:], COPY)
 
-        m1 = sb.tile([P, T], F32, name="m1")
-        nc.vector.tensor_tensor(m1[:], f1[:], f2[:], ALU.max)
+        def transpose_blocks(dst, src, n_blocks):
+            for i in range(n_blocks):
+                nc.tensor.transpose(dst[:, i * P : (i + 1) * P], src[:, i * P : (i + 1) * P], ident[:])
+
+        bank_runs = ((0, 2 * PAIR), (2 * PAIR, PAIR))
+        f2_turned = sb.tile([P, VECTOR_COLS], F32, name="f2_turned")
+        for b, (c0, n) in enumerate(bank_runs):
+            f2_ps = ps.tile([P, n], F32, name="f2_ps%d" % b, tag="bank%d" % b)
+            transpose_blocks(f2_ps[:], f2[:, c0 : c0 + n], n // P)
+            nc.vector.tensor_copy(f2_turned[:, c0 : c0 + n], f2_ps[:])
+        m1_ps = [ps.tile([P, n], F32, name="m1_ps%d" % b) for b, (c0, n) in enumerate(bank_runs)]
+        f1_ps = [
+            ps.tile([P, PAIR], F32, name="f1_ps%d" % g, tag="bank%d" % (len(bank_runs) + g))
+            for g in range(VECTOR_PAIRS)
+        ]
+        m1_turned = [sb.tile([P, PAIR], F32, name="m1_turned%d" % g) for g in range(VECTOR_PAIRS)]
+        for g in range(VECTOR_PAIRS):
+            transpose_blocks(f1_ps[g][:], f1[:, g * PAIR : (g + 1) * PAIR], 2)
+        for g in range(VECTOR_PAIRS):
+            nc.vector.tensor_tensor(m1_turned[g][:], f1_ps[g][:], f2_turned[:, g * PAIR : (g + 1) * PAIR], ALU.max)
+        for g in range(VECTOR_PAIRS):
+            transpose_blocks(m1_ps[g // 2][:, (g % 2) * PAIR : (g % 2 + 1) * PAIR], m1_turned[g][:], 2)
+        m1_rest = sb.tile([P, T - VECTOR_COLS], F32, name="m1_rest")
+        nc.vector.tensor_tensor(m1_rest[:], f1[:, VECTOR_COLS:T], f2[:, VECTOR_COLS:T], ALU.max)
+
         r = sb.tile([P, T], F32, name="r")
-        nc.vector.tensor_tensor(r[:], m1[:], f3[:], ALU.subtract)
+        nc.gpsimd.tensor_tensor(r[:, VECTOR_COLS:T], m1_rest[:], f3[:, VECTOR_COLS:T], ALU.subtract)
+        for b, (c0, n) in enumerate(bank_runs):
+            nc.vector.tensor_tensor(r[:, c0 : c0 + n], m1_ps[b][:], f3[:, c0 : c0 + n], ALU.subtract)
 
-        y0 = sb.tile([P, HALF], F32, name="y0")
-        y1 = sb.tile([P, HALF], F32, name="y1")
-        picked = sb.tile([P, HALF], F32, name="picked")
-        nc.scalar.activation(picked[:], r[:].indirect(half_list("idx6", 1)), COPY)
-        nc.vector.tensor_tensor(y0[:], r[:].indirect(half_list("idx6", 0)), g3[:, 0:HALF], ALU.add)
-        nc.sync.dma_start(out[:, 0:HALF], y0[:])
-        nc.vector.tensor_tensor(y1[:], picked[:], g3[:, HALF:SLOTS], ALU.add)
-        nc.sync.dma_start(out[:, HALF:SLOTS], y1[:])
+        y_first = sb.tile([P, HALF], F32, name="y_first")
+        y_second = sb.tile([P, HALF], F32, name="y_second")
+        r_second = sb.tile([P, HALF], F32, name="r_second")
+        nc.scalar.activation(r_second[:], r[:].indirect(half_list("idx6", 1)), COPY)
+        nc.vector.tensor_tensor(y_first[:], r[:].indirect(half_list("idx6", 0)), by_idx3[:, 0:HALF], ALU.add)
+        nc.sync.dma_start(out[:, 0:HALF], y_first[:])
+        nc.vector.tensor_tensor(y_second[:], r_second[:], by_idx3[:, HALF:SLOTS], ALU.add)
+        nc.sync.dma_start(out[:, HALF:SLOTS], y_second[:])

from contextlib import ExitStack

import concourse.mybir as mybir
from concourse.masks import make_identity

D, K, T, SLOTS, Q = 512, 512, 1024, 512, 128
FLOPS = 2 * D * K * Q + 2 * K * Q * T + 2 * D * Q * T

F32 = mybir.dt.float32
BF16 = mybir.dt.bfloat16
I32 = mybir.dt.int32
U32 = mybir.dt.uint32
U16 = mybir.dt.uint16
U8 = mybir.dt.uint8
FP8X4 = mybir.dt.float8_e4m3fn_x4
FP4X4 = mybir.dt.float4_e2m1fn_x4
COPY = mybir.ActivationFunctionType.Copy
ALU = mybir.AluOpType

P = 128
PACK = 4
QUADS = 4
QUAD = P // QUADS
LIVE = 4
TAGS_FIRST = 4
T_HALF = T // 2
BANK_COLS = (256, 256, 256, 128, 128)
HALF = SLOTS // 2
LIST_COLS = SLOTS // 16
PAIR = 2 * P
VECTOR_PAIRS = 3
VECTOR_COLS = VECTOR_PAIRS * PAIR


def tile_attend_threewrites_parts_kernel(
    tc, states, wq_words, wq_scales, cache_words, cache_scales, tags_words, tags_scales,
    offs, offs2, offs3, offs4, offs5, offs6, out,
):
    nc = tc.nc
    with ExitStack() as ctx:
        sb = ctx.enter_context(tc.tile_pool(name="sb", bufs=1))
        ps = ctx.enter_context(tc.psum_pool(name="ps", bufs=1))

        key_rows = sb.tile([P // 2, 2 * T], U8, name="key_rows", tag="rows_then_f2")
        nc.vector.memset(key_rows[:].bitcast(I32), 0)
        wq_spread = sb.tile([P, K], U8, name="wq_spread")
        nc.vector.memset(wq_spread[:].bitcast(I32), 0)

        wq_rows = sb.tile([LIVE, QUADS * K], U8, name="wq_rows")
        nc.sync.dma_start(
            wq_rows[:].bitcast(I32).rearrange("s (u n) -> s u n", u=QUADS),
            wq_scales[0].bitcast(I32).rearrange("(u s) n -> s u n", u=QUADS),
        )
        states_raw = sb.tile([P, PACK, Q], F32, name="states_raw")
        nc.sync.dma_start(states_raw[:], states.rearrange("(p j) q -> p j q", j=PACK))
        wq_raw = sb.tile([P, K], U32, name="wq_raw")
        nc.sync.dma_start(wq_raw[:].bitcast(I32), wq_words[0].rearrange("p n j -> p (n j)").bitcast(I32))
        for odd in range(2):
            for scales, first in ((tags_scales, TAGS_FIRST), (cache_scales, 0)):
                by_quad = scales[0].bitcast(I32).rearrange("(h o s) n -> o s h n", h=2, o=2)
                p0 = QUAD * odd + first
                nc.sync.dma_start(
                    key_rows[p0 : p0 + LIVE, :].bitcast(I32).rearrange("s (h n) -> s h n", h=2), by_quad[odd]
                )
        tags_flat = tags_words[0].rearrange("p n j -> p (n j)").bitcast(I32)
        tags_codes = []
        for h in range(2):
            codes = sb.tile([P, T_HALF], U32, name="tags_codes%d" % h, align_bytes=64)
            nc.sync.dma_start(codes[:].bitcast(I32), tags_flat[:, h * T_HALF : (h + 1) * T_HALF])
            tags_codes.append(codes)
        cache_codes = []
        for h in range(2):
            codes = sb.tile([P, 2 * T_HALF], U8, name="cache_codes%d" % h, align_bytes=64)
            nc.sync.dma_start(
                codes[:].bitcast(I32), cache_words[0][:, 2 * h * T_HALF : 2 * (h + 1) * T_HALF].bitcast(I32)
            )
            cache_codes.append(codes)
        lists = {}
        for name, src in (
            ("idx", offs), ("idx3", offs3), ("idx2", offs2), ("idx4", offs4), ("idx5", offs5), ("idx6", offs6),
        ):
            lists[name] = sb.tile([P, LIST_COLS], U16, name=name)
            nc.sync.dma_start(lists[name][:], src)

        f1 = sb.tile([P, T], F32, name="f1")
        nc.vector.memset(f1[:], 0.0)
        ident = sb.tile([P, P], F32, name="ident")
        make_identity(nc, ident[:])

        for u in range(QUADS):
            nc.vector.tensor_copy(
                wq_spread[QUAD * u : QUAD * u + LIVE, :].bitcast(I32),
                wq_rows[:, u * K : (u + 1) * K].bitcast(I32),
            )
        wq_plane = sb.tile([P, K], U8, name="wq_plane", align_bytes=64)
        nc.vector.tensor_copy(
            wq_plane[:].rearrange("p (j m) -> p m j", j=PACK),
            wq_spread[:].rearrange("p (m j) -> p m j", j=PACK),
        )

        states_bf = sb.tile([P, Q * PACK], BF16, name="states_bf", tag="states_then_planes", align_bytes=64)
        nc.scalar.activation(
            states_bf[:].rearrange("p (c i j) -> p c j i", i=4, j=PACK),
            states_raw[:].rearrange("p j (c i) -> p c j i", i=4),
            COPY,
        )
        wq_by_place = wq_raw[:].rearrange("p (m j) -> p m j", j=PACK)
        wq_dealt = [sb.tile([P, 2 * P], U32, name="wq_dealt%d" % h, align_bytes=64) for h in range(2)]
        for h in range(2):
            nc.scalar.copy(wq_dealt[h][:].rearrange("p (j m) -> p m j", j=2), wq_by_place[:, :, 2 * h : 2 * h + 2])

        states_codes = sb.tile([P, Q], U32, name="states_codes", align_bytes=64)
        states_plane = sb.tile([P, Q], U8, name="states_plane", align_bytes=64)
        nc.vector.quantize_mx(states_codes[:].bitcast(FP8X4), states_plane[:], states_bf[:])

        qv_ps = ps.tile([P, PACK * Q], F32, name="qv_ps")
        for j in range(PACK):
            nc.tensor.matmul_mx(
                qv_ps[:, j * Q : (j + 1) * Q],
                lhsT=wq_dealt[j // 2][:, (j % 2) * P : (j % 2 + 1) * P].bitcast(FP8X4),
                lhsT_scale=wq_plane[:, j * P : (j + 1) * P],
                rhs=states_codes[:].bitcast(FP8X4),
                rhs_scale=states_plane[:],
                start=True,
                stop=True,
            )
        qv_bf = sb.tile([P, Q * PACK], BF16, name="qv_bf", tag="qv_then_f3", align_bytes=64)
        nc.scalar.copy(
            qv_bf[:].rearrange("p (q j) -> p q j", j=PACK),
            qv_ps[:].rearrange("p (j q) -> p q j", j=PACK),
        )

        key_planes = sb.tile([P, T], U8, name="key_planes", tag="states_then_planes", align_bytes=64)
        for h in range(2):
            nc.vector.tensor_copy(
                key_planes[h * P // 2 : (h + 1) * P // 2, :].bitcast(I32),
                key_rows[:, h * T : (h + 1) * T].bitcast(I32),
            )
        f2 = sb.tile([P, T], F32, name="f2", tag="rows_then_f2")
        nc.vector.memset(f2[:], 0.0)

        qv_codes = sb.tile([P, Q], U32, name="qv_codes", align_bytes=64)
        qv_plane = sb.tile([P, Q], U8, name="qv_plane", align_bytes=64)
        nc.vector.quantize_mx(qv_codes[:].bitcast(FP8X4), qv_plane[:], qv_bf[:])

        f3 = sb.tile([P, T], F32, name="f3", tag="qv_then_f3", align_bytes=64)
        nc.vector.memset(f3[:], 0.0)

        starts = [sum(BANK_COLS[:b]) for b in range(len(BANK_COLS))]
        banks = [ps.tile([P, n], F32, name="score%d" % b, tag="bank%d" % b) for b, n in enumerate(BANK_COLS)]
        for bank, c0, n in zip(banks, starts, BANK_COLS):
            h, within = divmod(c0, T_HALF)
            nc.tensor.matmul_mx(
                bank[:],
                lhsT=states_codes[:].bitcast(FP8X4),
                lhsT_scale=states_plane[:],
                rhs=tags_codes[h][:, within : within + n].bitcast(FP8X4),
                rhs_scale=key_planes[TAGS_FIRST:P, c0 : c0 + n],
                start=True,
                stop=False,
            )
        a = sb.tile([P, T], F32, name="a")
        for b, (bank, c0, n) in enumerate(zip(banks, starts, BANK_COLS)):
            h, within = divmod(c0, T_HALF)
            nc.tensor.matmul_mx(
                bank[:],
                lhsT=qv_codes[:].bitcast(FP8X4),
                lhsT_scale=qv_plane[:],
                rhs=cache_codes[h][:, 2 * within : 2 * (within + n)].bitcast(FP4X4),
                rhs_scale=key_planes[:, c0 : c0 + n],
                start=False,
                stop=True,
            )
            if b % 2 == 1:
                nc.vector.tensor_copy(a[:, c0 : c0 + n], bank[:])
            else:
                nc.scalar.copy(a[:, c0 : c0 + n], bank[:])

        def half_list(name, h):
            return lists[name][:, h * LIST_COLS // 2 : (h + 1) * LIST_COLS // 2]

        by_idx3 = sb.tile([P, SLOTS], F32, name="by_idx3")
        by_idx5 = sb.tile([P, SLOTS], F32, name="by_idx5")
        by_idx_first = sb.tile([P, HALF], F32, name="by_idx_first", tag="by_idx")
        nc.vector.tensor_copy(by_idx_first[:], a[:].indirect(half_list("idx", 0)))
        nc.scalar.activation(f1[:].indirect(half_list("idx2", 0)), by_idx_first[:], COPY)
        nc.vector.tensor_copy(by_idx3[:], a[:].indirect(lists["idx3"][:]))
        nc.scalar.activation(f2[:].indirect(lists["idx4"][:]), by_idx3[:], COPY)
        by_idx_second = sb.tile([P, HALF], F32, name="by_idx_second", tag="by_idx")
        nc.vector.tensor_copy(by_idx_second[:], a[:].indirect(half_list("idx", 1)))
        nc.scalar.activation(f1[:].indirect(half_list("idx2", 1)), by_idx_second[:], COPY)
        nc.vector.tensor_copy(by_idx5[:], a[:].indirect(lists["idx5"][:]))
        nc.scalar.activation(f3[:].indirect(lists["idx"][:]), by_idx5[:], COPY)

        def transpose_blocks(dst, src, n_blocks):
            for i in range(n_blocks):
                nc.tensor.transpose(dst[:, i * P : (i + 1) * P], src[:, i * P : (i + 1) * P], ident[:])

        bank_runs = ((0, 2 * PAIR), (2 * PAIR, PAIR))
        f2_turned = sb.tile([P, VECTOR_COLS], F32, name="f2_turned")
        for b, (c0, n) in enumerate(bank_runs):
            f2_ps = ps.tile([P, n], F32, name="f2_ps%d" % b, tag="bank%d" % b)
            transpose_blocks(f2_ps[:], f2[:, c0 : c0 + n], n // P)
            nc.vector.tensor_copy(f2_turned[:, c0 : c0 + n], f2_ps[:])
        m1_ps = [ps.tile([P, n], F32, name="m1_ps%d" % b) for b, (c0, n) in enumerate(bank_runs)]
        f1_ps = [
            ps.tile([P, PAIR], F32, name="f1_ps%d" % g, tag="bank%d" % (len(bank_runs) + g))
            for g in range(VECTOR_PAIRS)
        ]
        m1_turned = [sb.tile([P, PAIR], F32, name="m1_turned%d" % g) for g in range(VECTOR_PAIRS)]
        for g in range(VECTOR_PAIRS):
            transpose_blocks(f1_ps[g][:], f1[:, g * PAIR : (g + 1) * PAIR], 2)
        for g in range(VECTOR_PAIRS):
            nc.vector.tensor_tensor(m1_turned[g][:], f1_ps[g][:], f2_turned[:, g * PAIR : (g + 1) * PAIR], ALU.max)
        for g in range(VECTOR_PAIRS):
            transpose_blocks(m1_ps[g // 2][:, (g % 2) * PAIR : (g % 2 + 1) * PAIR], m1_turned[g][:], 2)
        m1_rest = sb.tile([P, T - VECTOR_COLS], F32, name="m1_rest")
        nc.vector.tensor_tensor(m1_rest[:], f1[:, VECTOR_COLS:T], f2[:, VECTOR_COLS:T], ALU.max)

        r = sb.tile([P, T], F32, name="r")
        nc.gpsimd.tensor_tensor(r[:, VECTOR_COLS:T], m1_rest[:], f3[:, VECTOR_COLS:T], ALU.subtract)
        for b, (c0, n) in enumerate(bank_runs):
            nc.vector.tensor_tensor(r[:, c0 : c0 + n], m1_ps[b][:], f3[:, c0 : c0 + n], ALU.subtract)

        y_first = sb.tile([P, HALF], F32, name="y_first")
        y_second = sb.tile([P, HALF], F32, name="y_second")
        r_second = sb.tile([P, HALF], F32, name="r_second")
        nc.scalar.activation(r_second[:], r[:].indirect(half_list("idx6", 1)), COPY)
        nc.vector.tensor_tensor(y_first[:], r[:].indirect(half_list("idx6", 0)), by_idx3[:, 0:HALF], ALU.add)
        nc.sync.dma_start(out[:, 0:HALF], y_first[:])
        nc.vector.tensor_tensor(y_second[:], r_second[:], by_idx3[:, HALF:SLOTS], ALU.add)
        nc.sync.dma_start(out[:, HALF:SLOTS], y_second[:])
